import numpy as np
import ml_dtypes


def mxq(x, axis, fmt="e4m3"):
    dtype, down = {"e4m3": (ml_dtypes.float8_e4m3fn, 7), "e5m2": (ml_dtypes.float8_e5m2, 14)}[fmt]
    v = np.moveaxis(np.asarray(x, np.float32).astype(ml_dtypes.bfloat16).astype(np.float64), axis, -1)
    blocks = v.reshape(v.shape[:-1] + (-1, 32))
    amax = np.abs(blocks).max(-1, keepdims=True)
    byte = np.maximum(np.where(amax > 0, np.frexp(amax)[1] - 1 + 127, 0) - down, 1)
    scale = np.exp2(byte - 127.0)
    codes = (blocks / scale).astype(np.float32).astype(dtype).astype(np.float64)
    return np.moveaxis((codes * scale).reshape(v.shape), -1, axis)


WIDE = False


def mx_kscale(k):
    if not WIDE:
        return np.ones(k)
    levels = np.array([10, -10, 5, -5, 0])
    if k % 512:
        return np.exp2(np.random.permutation(np.resize(levels, k // 32))).repeat(32)
    a = np.empty((k // 512, 16))
    for p in range(k // 512):
        a[p, :8] = np.random.permutation(np.resize(levels, 8))
        for g in range(8):
            far = levels[np.abs(levels - a[p, g]) >= 10]
            a[p, g + 8] = far[np.random.randint(len(far))]
    return np.exp2(a.ravel()).repeat(32)


def f64(x):
    return np.asarray(x).astype(np.float64)


def striped(idx):
    return np.tile(np.asarray(idx).reshape(-1, 16).T, (8, 1)).astype(np.uint16)


def unstriped(offs):
    return offs[:16].T.reshape(-1).astype(np.int64)


def striped8(idx):
    return np.asarray(idx).reshape(8, -1, 16).transpose(0, 2, 1).reshape(128, -1).astype(np.uint16)


def unstriped8(offs):
    return offs.reshape(8, 16, -1).transpose(0, 2, 1).reshape(8, -1).astype(np.int64)


def pick8(x, idx, run):
    r = np.arange(len(x))
    return x[r[:, None], idx[r % (8 * run) // run]]


E2M1 = np.array([0.0, 0.5, 1.0, 1.5, 2.0, 3.0, 4.0, 6.0, -0.0, -0.5, -1.0, -1.5, -2.0, -3.0, -4.0, -6.0])


def pack_weight(w, fmt):
    k, n = w.shape
    w = f64(np.asarray(w, np.float32).astype(ml_dtypes.bfloat16)).reshape(k // 32, 32, n)
    amax = np.abs(w).max(1)
    if fmt == "e4m3":
        byte = np.frexp(amax)[1] - 1 + 127 - 7
    else:
        mant, ex = np.frexp(amax / 6.0)
        byte = np.where(mant > 0.5, ex, ex - 1) + 127
    byte = np.clip(np.where(amax > 0, byte, 1), 1, 254)
    scaled = (w * np.exp2(127.0 - byte)[:, None, :]).reshape(k, n).astype(np.float32)
    by_word = np.ascontiguousarray(scaled.reshape(k // 512, 128, 4, n).transpose(0, 1, 3, 2))
    if fmt == "e4m3":
        words = by_word.astype(ml_dtypes.float8_e4m3fn).view(np.uint8)
    else:
        c = by_word.astype(ml_dtypes.float4_e2m1fn).view(np.uint8) & 0xF
        words = (c[..., 0::2] | (c[..., 1::2] << 4)).reshape(k // 512, 128, 2 * n)
    return np.ascontiguousarray(words), np.ascontiguousarray(byte.astype(np.uint8).reshape(k // 512, 16, n))


def unpack_weight(words, scales, fmt):
    g, _, n = scales.shape
    words = np.ascontiguousarray(words).reshape(g, 128, n, -1)
    if fmt == "e4m3":
        vals = words.view(ml_dtypes.float8_e4m3fn).astype(np.float64)
    else:
        nib = np.empty((g, 128, n, 4), np.uint8)
        nib[..., 0::2] = words & 0xF
        nib[..., 1::2] = words >> 4
        vals = E2M1[nib]
    vals = vals * np.repeat(np.exp2(scales.astype(np.float64) - 127.0), 8, axis=1)[..., None]
    return vals.transpose(0, 1, 3, 2).reshape(g * 512, n)


K, J, R, T, F, O, C, N, U, E = 512, 512, 512, 1024, 1024, 192, 256, 256, 512, 128


def setup_inputs():
    n = np.random.standard_normal
    idx = np.random.permutation(T)[:J]
    idx2 = np.random.permutation(F)[:R]
    idx3 = np.stack([np.random.permutation(J)[:O] for _ in range(8)])
    idx4 = np.stack([np.random.permutation(C)[:O] for _ in range(8)])
    idx5 = np.stack([np.random.permutation(J)[:C] for _ in range(8)])
    idx6 = np.stack([np.random.permutation(U)[:C] for _ in range(8)])
    idx7 = np.stack([np.random.permutation(U)[:C] for _ in range(8)])
    fk = mx_kscale(K)
    fr = mx_kscale(R)
    tr = np.ones(F)
    tr[idx2] = fr
    xtp = pack_weight(n((K, T)) * fk[:, None], "e2m1")
    wtp = pack_weight(n((K, F)) * 1 / np.sqrt(K) / fk[:, None] * tr, "e2m1")
    wbp = pack_weight(n((R, N)) * 1 / np.sqrt(R) / fr[:, None], "e4m3")
    wop = pack_weight(n((R, N)) * 1 / np.sqrt(R) / fr[:, None], "e2m1")
    return {
        "xt_words": xtp[0],
        "xt_scales": xtp[1],
        "wt_words": wtp[0],
        "wt_scales": wtp[1],
        "sa": (np.random.uniform(0.5, 1.6, (R, 1))).astype(np.float32),
        "sb": (np.random.uniform(0.5, 1.6, (R, 1))).astype(np.float32),
        "wb_words": wbp[0],
        "wb_scales": wbp[1],
        "wo_words": wop[0],
        "wo_scales": wop[1],
        "offs": striped(idx),
        "offs2": striped(idx2),
        "offs3": striped8(idx3),
        "offs4": striped8(idx4),
        "offs5": striped8(idx5),
        "offs6": striped8(idx6),
        "offs7": striped8(idx7),
    }


def reference(xt_words, xt_scales, wt_words, wt_scales, sa, sb, wb_words, wb_scales, wo_words, wo_scales, offs, offs2, offs3, offs4, offs5, offs6, offs7):
    idx = unstriped(offs)
    idx2 = unstriped(offs2)
    idx3 = unstriped8(offs3)
    idx4 = unstriped8(offs4)
    idx5 = unstriped8(offs5)
    idx6 = unstriped8(offs6)
    idx7 = unstriped8(offs7)
    xtu = unpack_weight(xt_words, xt_scales, "e2m1")
    wtu = unpack_weight(wt_words, wt_scales, "e2m1")
    wbu = unpack_weight(wb_words, wb_scales, "e4m3")
    wou = unpack_weight(wo_words, wo_scales, "e2m1")
    wtidx2g = wtu[:, idx2]
    xtidxg = xtu[:, idx]
    a = wtidx2g.T @ xtidxg
    h1 = pick8(a, idx3, 64) * f64(sa)
    pw = np.zeros((R, C))
    pw[np.arange(R)[:, None], idx4[np.arange(R) % 512 // 64]] = h1
    hid = np.abs(pw - pick8(a, idx5, 64) * f64(sb))
    hidq = mxq(hid, 0, "e4m3")
    p = wbu.T @ hidq
    q = wou.T @ hidq
    m0 = np.zeros((N, U))
    m0[np.arange(N)[:, None], idx6[np.arange(N) % 128 // 16]] = p
    m1 = np.zeros((N, U))
    m1[np.arange(N)[:, None], idx7[np.arange(N) % 128 // 16]] = q
    m2 = m0.reshape(N, E, U // E).max(axis=2)
    m3 = m1.reshape(N, E, U // E).max(axis=2)
    y = m2 - m3
    return y

@@ -1,0 +1,204 @@
+from contextlib import ExitStack
+
+import concourse.mybir as mybir
+
+K, J, R, T, F, O, C, N, U, E = 512, 512, 512, 1024, 1024, 192, 256, 256, 512, 128
+FLOPS = 2 * K * R * J + 2 * 2 * R * N * C
+
+F32 = mybir.dt.float32
+BF16 = mybir.dt.bfloat16
+I32 = mybir.dt.int32
+U32 = mybir.dt.uint32
+U16 = mybir.dt.uint16
+U8 = mybir.dt.uint8
+FP8X4 = mybir.dt.float8_e4m3fn_x4
+FP4X4 = mybir.dt.float4_e2m1fn_x4
+ALU = mybir.AluOpType
+COPY = mybir.ActivationFunctionType.Copy
+
+P = 128
+PACK = 4
+HALF = C // 2
+JH = J // 2
+
+
+def tile_picked_tokens_store_one_wholepage_outcomes_endgap_kernel(
+    tc, xt_words, xt_scales, wt_words, wt_scales, sa, sb, wb_words, wb_scales, wo_words, wo_scales,
+    offs, offs2, offs3, offs4, offs5, offs6, offs7, out,
+):
+    nc = tc.nc
+    with ExitStack() as ctx:
+        lists = ctx.enter_context(tc.tile_pool(name="lists", bufs=1))
+        keep = ctx.enter_context(tc.tile_pool(name="keep", bufs=1))
+        psum = ctx.enter_context(tc.psum_pool(name="psum", bufs=1))
+
+        def sbuf(name, cols, dtype, tag=""):
+            return keep.tile([P, cols], dtype, name=name, tag=tag or name, align_bytes=64)
+
+        def load_list(name, src):
+            tile = lists.tile([P, src.shape[1]], U16, name=name)
+            nc.sync.dma_start(tile[:], src)
+            return tile
+
+        def load_bytes(tile, src):
+            nc.sync.dma_start(tile[:].bitcast(I32), src.bitcast(I32))
+
+        def load_scale_rows(tile, src):
+            for q in range(4):
+                nc.sync.dma_start(tile[32 * q : 32 * q + 4, :].bitcast(I32), src[0, 4 * q : 4 * q + 4, :].bitcast(I32))
+
+        wt_win = sbuf("wt_win", F, U16)
+        wts_win = sbuf("wts_win", F, U8)
+        xt_win = sbuf("xt_win", T, U16)
+        xts_win = sbuf("xts_win", T, U8)
+        wb_w = sbuf("wb_w", N, U32)
+        wb_s = sbuf("wb_s", N, U8)
+        wo_w = sbuf("wo_w", N, U16)
+        wo_s = sbuf("wo_s", N, U8)
+        sa_t = sbuf("sa_t", PACK, F32)
+        sb_t = sbuf("sb_t", PACK, F32)
+        page = [sbuf("page%d" % t, C, F32) for t in range(PACK)]
+        m0 = [sbuf("m0_%d" % b, U, F32) for b in range(2)]
+        m1 = [sbuf("m1_%d" % b, U, F32) for b in range(2)]
+
+        for tile in (wts_win, xts_win, wb_s, wo_s):
+            nc.vector.memset(tile[:].bitcast(I32), 0)
+        for tile in page + m0 + m1:
+            nc.vector.memset(tile[:], 0.0)
+
+        l2 = load_list("l2", offs2)
+        load_bytes(wt_win, wt_words[0])
+        load_scale_rows(wts_win, wt_scales)
+        l1 = load_list("l1", offs)
+        load_bytes(xt_win, xt_words[0])
+        load_scale_rows(xts_win, xt_scales)
+        l3 = load_list("l3", offs3)
+        nc.sync.dma_start(sa_t[:], sa.rearrange("(p t) o -> p (t o)", t=PACK))
+        l5 = load_list("l5", offs5)
+        nc.sync.dma_start(sb_t[:], sb.rearrange("(p t) o -> p (t o)", t=PACK))
+        l4 = load_list("l4", offs4)
+        load_bytes(wb_w, wb_words[0].rearrange("p n t -> p (n t)"))
+        load_scale_rows(wb_s, wb_scales)
+        l6 = load_list("l6", offs6)
+        load_bytes(wo_w, wo_words[0])
+        load_scale_rows(wo_s, wo_scales)
+        l7 = load_list("l7", offs7)
+
+        wt_g = sbuf("wt_g", R, U16)
+        wts_g = sbuf("wts_g", R, U8)
+        xt_g = sbuf("xt_g", J, U16)
+        xts_g = sbuf("xts_g", J, U8)
+        nc.vector.tensor_copy(wt_g[:], wt_win[:].indirect(l2[:]))
+        nc.vector.tensor_copy(wts_g[:], wts_win[:].indirect(l2[:]))
+        nc.vector.tensor_copy(xt_g[:], xt_win[:].indirect(l1[:]))
+
+        def deal(t):
+            words = sbuf("wt_d%d" % t, 2 * P, U8)
+            scales = sbuf("wts_d%d" % t, P, U8)
+            nc.vector.tensor_copy(
+                words[:].rearrange("p (m b) -> p m b", b=2),
+                wt_g[:].bitcast(U8).rearrange("p (m t b) -> p m t b", t=PACK, b=2)[:, :, t, :],
+            )
+            nc.vector.tensor_copy(scales[:], wts_g[:].rearrange("p (m t) -> p m t", t=PACK)[:, :, t])
+            return words, scales
+
+        def first_product(acc, lhs, cols):
+            nc.tensor.matmul_mx(
+                out=acc, lhsT=lhs[0][:].bitcast(FP4X4), lhsT_scale=lhs[1][:],
+                rhs=xt_g[:, cols].bitcast(FP4X4), rhs_scale=xts_g[:, cols], start=True, stop=True,
+            )
+
+        a = [sbuf("a%d" % t, J, F32) for t in range(PACK)]
+        lhs0 = deal(0)
+        for s in range(2):
+            cols = slice(s * JH, (s + 1) * JH)
+            nc.vector.tensor_copy(xts_g[:, cols], xts_win[:].indirect(l1[:, s * JH // 16 : (s + 1) * JH // 16]))
+            acc = psum.tile([P, JH], F32, name="acc0_%d" % s)
+            first_product(acc[:], lhs0, cols)
+            nc.scalar.copy(a[0][:, cols], acc[:])
+
+        hid = [sbuf("hid%d" % s, PACK * HALF, BF16) for s in range(2)]
+        codes = sbuf("codes", C, U32)
+        planes = sbuf("planes", C, U8)
+
+        def second_fetch(dst, t, s):
+            nc.scalar.activation(
+                out=dst, in_=a[t][:].indirect(l5[:, s * HALF // 16 : (s + 1) * HALF // 16]), func=COPY,
+                scale=sb_t[:, t : t + 1],
+            )
+
+        for t in range(PACK):
+            if t > 0:
+                lhs = deal(t)
+                acc = psum.tile([P, J], F32, name="acc%d" % t)
+                first_product(acc[:], lhs, slice(0, J))
+                nc.vector.tensor_copy(a[t][:], acc[:])
+            h1 = sbuf("h1_%d" % t, O, F32, tag="late" if t == PACK - 1 else "")
+            nc.scalar.activation(out=h1[:], in_=a[t][:].indirect(l3[:]), func=COPY, scale=sa_t[:, t : t + 1])
+            g = sbuf("gA%d" % t, HALF, F32)
+            second_fetch(g[:], t, 0)
+            nc.scalar.activation(out=page[t][:].indirect(l4[:]), in_=h1[:], func=COPY)
+            d = sbuf("dA%d" % t, HALF, F32)
+            nc.vector.tensor_tensor(d[:], page[t][:, 0:HALF], g[:], ALU.subtract)
+            nc.vector.scalar_tensor_tensor(
+                out=hid[0][:].rearrange("p (c t) -> p c t", t=PACK)[:, :, t], in0=d[:], scalar=-1.0, in1=d[:],
+                op0=ALU.mult, op1=ALU.max,
+            )
+
+        gB = sbuf("gB", PACK * HALF, F32, tag="late")
+        for t in range(PACK):
+            second_fetch(gB[:, t * HALF : (t + 1) * HALF], t, 1)
+
+        outcomes = [(wb_w, wb_s, FP8X4, m0, l6), (wo_w, wo_s, FP4X4, m1, l7)]
+
+        def second_products(s):
+            cols = slice(s * HALF, (s + 1) * HALF)
+            nc.vector.quantize_mx(out=codes[:, cols].bitcast(FP8X4), scales=planes[:, cols], in_=hid[s][:])
+            staged = []
+            for b in range(2):
+                rows = slice(b * P, (b + 1) * P)
+                for i, (words, scales, fmt, pages, lst) in enumerate(outcomes):
+                    first = s == 0 and b == 0 and i == 0
+                    acc = psum.tile([P, HALF], F32, name="res%d%d%d" % (s, b, i), tag="acc%d" % (1 + (2 * b + i) % 3) if not first else "first")
+                    nc.tensor.matmul_mx(
+                        out=acc[:], lhsT=words[:, rows].bitcast(fmt), lhsT_scale=scales[:, rows],
+                        rhs=codes[:, cols].bitcast(FP8X4), rhs_scale=planes[:, cols], start=True, stop=True,
+                    )
+                    res = sbuf("res_sb%d%d%d" % (s, b, i), HALF, F32)
+                    nc.vector.tensor_copy(res[:], acc[:])
+                    staged.append((res, pages[b], lst))
+            return staged
+
+        def put(staged, s):
+            res, window, lst = staged
+            nc.scalar.activation(
+                out=window[:].indirect(lst[:, s * HALF // 16 : (s + 1) * HALF // 16]), in_=res[:], func=COPY
+            )
+
+        stagedA = second_products(0)
+        dB = sbuf("dB", PACK * HALF, F32)
+        for t in range(PACK):
+            cols = slice(t * HALF, (t + 1) * HALF)
+            nc.vector.tensor_tensor(dB[:, cols], page[t][:, HALF:C], gB[:, cols], ALU.subtract)
+        dB_ct = dB[:].rearrange("p (t c) -> p c t", t=PACK)
+        nc.vector.scalar_tensor_tensor(
+            out=hid[1][:].rearrange("p (c t) -> p c t", t=PACK), in0=dB_ct, scalar=-1.0, in1=dB_ct,
+            op0=ALU.mult, op1=ALU.max,
+        )
+        for item in stagedA:
+            put(item, 0)
+        stagedB = second_products(1)
+        for b in range(2):
+            tops = []
+            for i in range(2):
+                item = stagedB[2 * b + i]
+                put(item, 1)
+                top = sbuf("top%d%d" % (b, i), E, F32)
+                nc.vector.tensor_reduce(
+                    out=top[:], in_=item[1][:].rearrange("p (e u) -> p e u", u=U // E),
+                    axis=mybir.AxisListType.X, op=ALU.max,
+                )
+                tops.append(top)
+            y = sbuf("y%d" % b, E, F32)
+            nc.vector.tensor_tensor(y[:], tops[0][:], tops[1][:], ALU.subtract)
+            nc.sync.dma_start(out[b * P : (b + 1) * P, :], y[:])

@@ -30,6 +30,7 @@ def tile_picked_tokens_store_one_wholepage_outcomes_endgap_kernel(
     with ExitStack() as ctx:
         lists = ctx.enter_context(tc.tile_pool(name="lists", bufs=1))
         keep = ctx.enter_context(tc.tile_pool(name="keep", bufs=1))
+        reuse = ctx.enter_context(tc.tile_pool(name="reuse", bufs=1))
         psum = ctx.enter_context(tc.psum_pool(name="psum", bufs=1))
 
         def sbuf(name, cols, dtype, tag=""):
@@ -47,10 +48,17 @@ def tile_picked_tokens_store_one_wholepage_outcomes_endgap_kernel(
             for q in range(4):
                 nc.sync.dma_start(tile[32 * q : 32 * q + 4, :].bitcast(I32), src[0, 4 * q : 4 * q + 4, :].bitcast(I32))
 
+        def load_scale_window(tile, src):
+            for q in range(4):
+                rows = src[0, 4 * q : 4 * q + 4, :].bitcast(I32)
+                nc.sync.dma_start(
+                    tile[32 * q : 32 * q + 32, :].bitcast(I32), rows.unsqueeze(0).broadcast_to([8, 4, rows.shape[1]])
+                )
+
         wt_win = sbuf("wt_win", F, U16)
         wts_win = sbuf("wts_win", F, U8)
         xt_win = sbuf("xt_win", T, U16)
-        xts_win = sbuf("xts_win", T, U8)
+        xts_win = reuse.tile([P, T], U8, name="xts_win", align_bytes=64, offset=0)
         wb_w = sbuf("wb_w", N, U32)
         wb_s = sbuf("wb_s", N, U8)
         wo_w = sbuf("wo_w", N, U16)
@@ -61,17 +69,19 @@ def tile_picked_tokens_store_one_wholepage_outcomes_endgap_kernel(
         m0 = [sbuf("m0_%d" % b, U, F32) for b in range(2)]
         m1 = [sbuf("m1_%d" % b, U, F32) for b in range(2)]
 
-        for tile in (wts_win, xts_win, wb_s, wo_s):
+        for tile in (wb_s, wo_s):
             nc.vector.memset(tile[:].bitcast(I32), 0)
-        for tile in page + m0 + m1:
+        for tile in page + m0:
+            nc.gpsimd.memset(tile[:], 0.0)
+        for tile in m1:
             nc.vector.memset(tile[:], 0.0)
 
         l2 = load_list("l2", offs2)
+        load_scale_window(wts_win, wt_scales)
         load_bytes(wt_win, wt_words[0])
-        load_scale_rows(wts_win, wt_scales)
         l1 = load_list("l1", offs)
         load_bytes(xt_win, xt_words[0])
-        load_scale_rows(xts_win, xt_scales)
+        load_scale_window(xts_win, xt_scales)
         l3 = load_list("l3", offs3)
         nc.sync.dma_start(sa_t[:], sa.rearrange("(p t) o -> p (t o)", t=PACK))
         l5 = load_list("l5", offs5)
@@ -88,17 +98,18 @@ def tile_picked_tokens_store_one_wholepage_outcomes_endgap_kernel(
         wts_g = sbuf("wts_g", R, U8)
         xt_g = sbuf("xt_g", J, U16)
         xts_g = sbuf("xts_g", J, U8)
-        nc.vector.tensor_copy(wt_g[:], wt_win[:].indirect(l2[:]))
         nc.vector.tensor_copy(wts_g[:], wts_win[:].indirect(l2[:]))
+        nc.vector.tensor_copy(wt_g[:], wt_win[:].indirect(l2[:]))
         nc.vector.tensor_copy(xt_g[:], xt_win[:].indirect(l1[:]))
 
         def deal(t):
-            words = sbuf("wt_d%d" % t, 2 * P, U8)
-            scales = sbuf("wts_d%d" % t, P, U8)
-            nc.vector.tensor_copy(
-                words[:].rearrange("p (m b) -> p m b", b=2),
-                wt_g[:].bitcast(U8).rearrange("p (m t b) -> p m t b", t=PACK, b=2)[:, :, t, :],
-            )
+            if t == 0:
+                words = sbuf("wt_d0", 2 * P, U8)
+                scales = sbuf("wts_d0", P, U8)
+            else:
+                scales = reuse.tile([P, P], U8, name="wts_d%d" % t, align_bytes=64, offset=(t - 1) * P)
+                words = reuse.tile([P, 2 * P], U8, name="wt_d%d" % t, align_bytes=64, offset=3 * P + (t - 1) * 2 * P)
+            nc.vector.tensor_copy(words[:].bitcast(U16), wt_g[:].rearrange("p (m t) -> p m t", t=PACK)[:, :, t])
             nc.vector.tensor_copy(scales[:], wts_g[:].rearrange("p (m t) -> p m t", t=PACK)[:, :, t])
             return words, scales
 
@@ -117,7 +128,7 @@ def tile_picked_tokens_store_one_wholepage_outcomes_endgap_kernel(
             first_product(acc[:], lhs0, cols)
             nc.scalar.copy(a[0][:, cols], acc[:])
 
-        hid = [sbuf("hid%d" % s, PACK * HALF, BF16) for s in range(2)]
+        hid = [sbuf("hid%d" % s, PACK * HALF, BF16, tag="diff" if s == 0 else "") for s in range(2)]
         codes = sbuf("codes", C, U32)
         planes = sbuf("planes", C, U8)
 
@@ -127,12 +138,13 @@ def tile_picked_tokens_store_one_wholepage_outcomes_endgap_kernel(
                 scale=sb_t[:, t : t + 1],
             )
 
+        for t in range(1, PACK):
+            lhs = deal(t)
+            acc = psum.tile([P, J], F32, name="acc%d" % t)
+            first_product(acc[:], lhs, slice(0, J))
+            nc.vector.tensor_copy(a[t][:], acc[:])
+
         for t in range(PACK):
-            if t > 0:
-                lhs = deal(t)
-                acc = psum.tile([P, J], F32, name="acc%d" % t)
-                first_product(acc[:], lhs, slice(0, J))
-                nc.vector.tensor_copy(a[t][:], acc[:])
             h1 = sbuf("h1_%d" % t, O, F32, tag="late" if t == PACK - 1 else "")
             nc.scalar.activation(out=h1[:], in_=a[t][:].indirect(l3[:]), func=COPY, scale=sa_t[:, t : t + 1])
             g = sbuf("gA%d" % t, HALF, F32)
@@ -149,56 +161,77 @@ def tile_picked_tokens_store_one_wholepage_outcomes_endgap_kernel(
         for t in range(PACK):
             second_fetch(gB[:, t * HALF : (t + 1) * HALF], t, 1)
 
-        outcomes = [(wb_w, wb_s, FP8X4, m0, l6), (wo_w, wo_s, FP4X4, m1, l7)]
+        first = (wb_w, wb_s, FP8X4, m0, l6)
+        second = (wo_w, wo_s, FP4X4, m1, l7)
 
-        def second_products(s):
+        def quantise(s):
             cols = slice(s * HALF, (s + 1) * HALF)
             nc.vector.quantize_mx(out=codes[:, cols].bitcast(FP8X4), scales=planes[:, cols], in_=hid[s][:])
-            staged = []
-            for b in range(2):
-                rows = slice(b * P, (b + 1) * P)
-                for i, (words, scales, fmt, pages, lst) in enumerate(outcomes):
-                    first = s == 0 and b == 0 and i == 0
-                    acc = psum.tile([P, HALF], F32, name="res%d%d%d" % (s, b, i), tag="acc%d" % (1 + (2 * b + i) % 3) if not first else "first")
-                    nc.tensor.matmul_mx(
-                        out=acc[:], lhsT=words[:, rows].bitcast(fmt), lhsT_scale=scales[:, rows],
-                        rhs=codes[:, cols].bitcast(FP8X4), rhs_scale=planes[:, cols], start=True, stop=True,
-                    )
-                    res = sbuf("res_sb%d%d%d" % (s, b, i), HALF, F32)
-                    nc.vector.tensor_copy(res[:], acc[:])
-                    staged.append((res, pages[b], lst))
-            return staged
 
-        def put(staged, s):
-            res, window, lst = staged
-            nc.scalar.activation(
-                out=window[:].indirect(lst[:, s * HALF // 16 : (s + 1) * HALF // 16]), in_=res[:], func=COPY
+        def product(outcome, b, cols, acc):
+            words, scales, fmt = outcome[:3]
+            rows = slice(b * P, (b + 1) * P)
+            nc.tensor.matmul_mx(
+                out=acc, lhsT=words[:, rows].bitcast(fmt), lhsT_scale=scales[:, rows],
+                rhs=codes[:, cols].bitcast(FP8X4), rhs_scale=planes[:, cols], start=True, stop=True,
             )
 
-        stagedA = second_products(0)
-        dB = sbuf("dB", PACK * HALF, F32)
+        def put(outcome, b, cols, res):
+            window, lst = outcome[3][b], outcome[4]
+            nc.scalar.activation(
+                out=window[:].indirect(lst[:, cols.start // 16 : cols.stop // 16]), in_=res, func=COPY
+            )
+
+        def bucket_tops(outcome, b, name):
+            top = sbuf(name, E, F32)
+            nc.vector.tensor_reduce(
+                out=top[:], in_=outcome[3][b][:].rearrange("p (e u) -> p e u", u=U // E),
+                axis=mybir.AxisListType.X, op=ALU.max,
+            )
+            return top
+
+        left, right, whole = slice(0, HALF), slice(HALF, C), slice(0, C)
+        early = [(first, 0), (second, 0), (first, 1)]
+        quantise(0)
+        accs = [psum.tile([P, HALF], F32, name="early%d" % i) for i in range(len(early))]
+        for acc, (o, b) in zip(accs, early):
+            product(o, b, left, acc[:])
+        lead = sbuf("lead", HALF, F32)
+        nc.scalar.copy(lead[:], accs[0][:])
+        put(first, 0, left, lead[:])
+
+        dB = sbuf("dB", PACK * HALF, F32, tag="diff")
         for t in range(PACK):
             cols = slice(t * HALF, (t + 1) * HALF)
-            nc.vector.tensor_tensor(dB[:, cols], page[t][:, HALF:C], gB[:, cols], ALU.subtract)
+            nc.vector.tensor_tensor(dB[:, cols], page[t][:, right], gB[:, cols], ALU.subtract)
         dB_ct = dB[:].rearrange("p (t c) -> p c t", t=PACK)
         nc.vector.scalar_tensor_tensor(
             out=hid[1][:].rearrange("p (c t) -> p c t", t=PACK), in0=dB_ct, scalar=-1.0, in1=dB_ct,
             op0=ALU.mult, op1=ALU.max,
         )
-        for item in stagedA:
-            put(item, 0)
-        stagedB = second_products(1)
-        for b in range(2):
-            tops = []
-            for i in range(2):
-                item = stagedB[2 * b + i]
-                put(item, 1)
-                top = sbuf("top%d%d" % (b, i), E, F32)
-                nc.vector.tensor_reduce(
-                    out=top[:], in_=item[1][:].rearrange("p (e u) -> p e u", u=U // E),
-                    axis=mybir.AxisListType.X, op=ALU.max,
-                )
-                tops.append(top)
-            y = sbuf("y%d" % b, E, F32)
-            nc.vector.tensor_tensor(y[:], tops[0][:], tops[1][:], ALU.subtract)
-            nc.sync.dma_start(out[b * P : (b + 1) * P, :], y[:])
+        resA = sbuf("resA", 2 * HALF, F32, tag="late")
+        nc.vector.tensor_copy(resA[:, left], accs[1][:])
+        put(second, 0, left, resA[:, left])
+        quantise(1)
+        nc.vector.tensor_copy(resA[:, right], accs[2][:])
+        put(first, 1, left, resA[:, right])
+
+        accB = psum.tile([P, len(early) * HALF], F32, name="accB", tag="acc1")
+        for i, (o, b) in enumerate(early):
+            product(o, b, right, accB[:, i * HALF : (i + 1) * HALF])
+        resB = sbuf("resB", len(early) * HALF, F32)
+        nc.vector.tensor_copy(resB[:], accB[:])
+        accW = psum.tile([P, C], F32, name="accW", tag="acc2")
+        product(second, 1, whole, accW[:])
+        resW = sbuf("resW", C, F32)
+        nc.vector.tensor_copy(resW[:], accW[:])
+
+        late = [(o, b, right, resB[:, i * HALF : (i + 1) * HALF]) for i, (o, b) in enumerate(early)]
+        tops = []
+        for i, (o, b, cols, res) in enumerate(late + [(second, 1, whole, resW[:])]):
+            put(o, b, cols, res)
+            tops.append(bucket_tops(o, b, "top%d" % i))
+            if o is second:
+                y = sbuf("y%d" % b, E, F32)
+                nc.vector.tensor_tensor(y[:], tops[-2][:], tops[-1][:], ALU.subtract)
+                nc.sync.dma_start(out[b * P : (b + 1) * P, :], y[:])

@@ -20,6 +20,7 @@ P = 128
 PACK = 4
 HALF = C // 2
 JH = J // 2
+PAGE_BYTES = 4 * C
 
 
 def tile_picked_tokens_store_one_wholepage_outcomes_endgap_kernel(
@@ -57,31 +58,33 @@ def tile_picked_tokens_store_one_wholepage_outcomes_endgap_kernel(
 
         wt_win = sbuf("wt_win", F, U16)
         wts_win = sbuf("wts_win", F, U8)
-        xt_win = sbuf("xt_win", T, U16)
-        xts_win = reuse.tile([P, T], U8, name="xts_win", align_bytes=64, offset=0)
+        xt_win = reuse.tile([P, T], U16, name="xt_win", align_bytes=64, offset=PAGE_BYTES - 2 * P)
+        xts_win = sbuf("xts_win", T, U8)
         wb_w = sbuf("wb_w", N, U32)
         wb_s = sbuf("wb_s", N, U8)
         wo_w = sbuf("wo_w", N, U16)
         wo_s = sbuf("wo_s", N, U8)
         sa_t = sbuf("sa_t", PACK, F32)
         sb_t = sbuf("sb_t", PACK, F32)
-        page = [sbuf("page%d" % t, C, F32) for t in range(PACK)]
+        page = [
+            reuse.tile([P, C], F32, name="page%d" % t, align_bytes=64, offset=t * PAGE_BYTES) for t in range(PACK)
+        ]
         m0 = [sbuf("m0_%d" % b, U, F32) for b in range(2)]
         m1 = [sbuf("m1_%d" % b, U, F32) for b in range(2)]
 
         for tile in (wb_s, wo_s):
             nc.vector.memset(tile[:].bitcast(I32), 0)
-        for tile in page + m0:
+        for tile in m0:
             nc.gpsimd.memset(tile[:], 0.0)
-        for tile in m1:
+        for tile in page[-1:] + m1:
             nc.vector.memset(tile[:], 0.0)
 
         l2 = load_list("l2", offs2)
         load_scale_window(wts_win, wt_scales)
         load_bytes(wt_win, wt_words[0])
         l1 = load_list("l1", offs)
-        load_bytes(xt_win, xt_words[0])
         load_scale_window(xts_win, xt_scales)
+        load_bytes(xt_win, xt_words[0])
         l3 = load_list("l3", offs3)
         nc.sync.dma_start(sa_t[:], sa.rearrange("(p t) o -> p (t o)", t=PACK))
         l5 = load_list("l5", offs5)
@@ -100,15 +103,15 @@ def tile_picked_tokens_store_one_wholepage_outcomes_endgap_kernel(
         xts_g = sbuf("xts_g", J, U8)
         nc.vector.tensor_copy(wts_g[:], wts_win[:].indirect(l2[:]))
         nc.vector.tensor_copy(wt_g[:], wt_win[:].indirect(l2[:]))
-        nc.vector.tensor_copy(xt_g[:], xt_win[:].indirect(l1[:]))
+        nc.vector.tensor_copy(xts_g[:], xts_win[:].indirect(l1[:]))
 
         def deal(t):
             if t == 0:
                 words = sbuf("wt_d0", 2 * P, U8)
                 scales = sbuf("wts_d0", P, U8)
             else:
-                scales = reuse.tile([P, P], U8, name="wts_d%d" % t, align_bytes=64, offset=(t - 1) * P)
-                words = reuse.tile([P, 2 * P], U8, name="wt_d%d" % t, align_bytes=64, offset=3 * P + (t - 1) * 2 * P)
+                scales = reuse.tile([P, P], U8, name="wts_d%d" % t, align_bytes=64, offset=2 * PAGE_BYTES + (t + 1) * P)
+                words = reuse.tile([P, 2 * P], U8, name="wt_d%d" % t, align_bytes=64, offset=max(PAGE_BYTES - 2 * P, (t - 1) * PAGE_BYTES))
             nc.vector.tensor_copy(words[:].bitcast(U16), wt_g[:].rearrange("p (m t) -> p m t", t=PACK)[:, :, t])
             nc.vector.tensor_copy(scales[:], wts_g[:].rearrange("p (m t) -> p m t", t=PACK)[:, :, t])
             return words, scales
@@ -123,7 +126,7 @@ def tile_picked_tokens_store_one_wholepage_outcomes_endgap_kernel(
         lhs0 = deal(0)
         for s in range(2):
             cols = slice(s * JH, (s + 1) * JH)
-            nc.vector.tensor_copy(xts_g[:, cols], xts_win[:].indirect(l1[:, s * JH // 16 : (s + 1) * JH // 16]))
+            nc.vector.tensor_copy(xt_g[:, cols], xt_win[:].indirect(l1[:, s * JH // 16 : (s + 1) * JH // 16]))
             acc = psum.tile([P, JH], F32, name="acc0_%d" % s)
             first_product(acc[:], lhs0, cols)
             nc.scalar.copy(a[0][:, cols], acc[:])
@@ -143,12 +146,20 @@ def tile_picked_tokens_store_one_wholepage_outcomes_endgap_kernel(
             acc = psum.tile([P, J], F32, name="acc%d" % t)
             first_product(acc[:], lhs, slice(0, J))
             nc.vector.tensor_copy(a[t][:], acc[:])
+            nc.vector.memset(page[t - 1][:], 0.0)
 
-        for t in range(PACK):
+        def first_fetch(t):
             h1 = sbuf("h1_%d" % t, O, F32, tag="late" if t == PACK - 1 else "")
             nc.scalar.activation(out=h1[:], in_=a[t][:].indirect(l3[:]), func=COPY, scale=sa_t[:, t : t + 1])
+            return h1
+
+        ahead = first_fetch(0)
+        for t in range(PACK):
+            h1 = ahead
             g = sbuf("gA%d" % t, HALF, F32)
             second_fetch(g[:], t, 0)
+            if t + 1 < PACK:
+                ahead = first_fetch(t + 1)
             nc.scalar.activation(out=page[t][:].indirect(l4[:]), in_=h1[:], func=COPY)
             d = sbuf("dA%d" % t, HALF, F32)
             nc.vector.tensor_tensor(d[:], page[t][:, 0:HALF], g[:], ALU.subtract)

from contextlib import ExitStack

import concourse.mybir as mybir

K, J, R, T, F, O, C, N, U, E = 512, 512, 512, 1024, 1024, 192, 256, 256, 512, 128
FLOPS = 2 * K * R * J + 2 * 2 * R * N * C

F32 = mybir.dt.float32
BF16 = mybir.dt.bfloat16
I32 = mybir.dt.int32
U32 = mybir.dt.uint32
U16 = mybir.dt.uint16
U8 = mybir.dt.uint8
FP8X4 = mybir.dt.float8_e4m3fn_x4
FP4X4 = mybir.dt.float4_e2m1fn_x4
ALU = mybir.AluOpType
COPY = mybir.ActivationFunctionType.Copy

P = 128
PACK = 4
HALF = C // 2
JH = J // 2
PAGE_BYTES = 4 * C


def tile_picked_tokens_store_one_wholepage_outcomes_endgap_kernel(
    tc, xt_words, xt_scales, wt_words, wt_scales, sa, sb, wb_words, wb_scales, wo_words, wo_scales,
    offs, offs2, offs3, offs4, offs5, offs6, offs7, out,
):
    nc = tc.nc
    with ExitStack() as ctx:
        lists = ctx.enter_context(tc.tile_pool(name="lists", bufs=1))
        keep = ctx.enter_context(tc.tile_pool(name="keep", bufs=1))
        reuse = ctx.enter_context(tc.tile_pool(name="reuse", bufs=1))
        psum = ctx.enter_context(tc.psum_pool(name="psum", bufs=1))

        def sbuf(name, cols, dtype, tag=""):
            return keep.tile([P, cols], dtype, name=name, tag=tag or name, align_bytes=64)

        def load_list(name, src):
            tile = lists.tile([P, src.shape[1]], U16, name=name)
            nc.sync.dma_start(tile[:], src)
            return tile

        def load_bytes(tile, src):
            nc.sync.dma_start(tile[:].bitcast(I32), src.bitcast(I32))

        def load_scale_rows(tile, src):
            for q in range(4):
                nc.sync.dma_start(tile[32 * q : 32 * q + 4, :].bitcast(I32), src[0, 4 * q : 4 * q + 4, :].bitcast(I32))

        def load_scale_window(tile, src):
            for q in range(4):
                rows = src[0, 4 * q : 4 * q + 4, :].bitcast(I32)
                nc.sync.dma_start(
                    tile[32 * q : 32 * q + 32, :].bitcast(I32), rows.unsqueeze(0).broadcast_to([8, 4, rows.shape[1]])
                )

        wt_win = sbuf("wt_win", F, U16)
        wts_win = sbuf("wts_win", F, U8)
        xt_win = reuse.tile([P, T], U16, name="xt_win", align_bytes=64, offset=PAGE_BYTES - 2 * P)
        xts_win = sbuf("xts_win", T, U8)
        wb_w = sbuf("wb_w", N, U32)
        wb_s = sbuf("wb_s", N, U8)
        wo_w = sbuf("wo_w", N, U16)
        wo_s = sbuf("wo_s", N, U8)
        sa_t = sbuf("sa_t", PACK, F32)
        sb_t = sbuf("sb_t", PACK, F32)
        page = [
            reuse.tile([P, C], F32, name="page%d" % t, align_bytes=64, offset=t * PAGE_BYTES) for t in range(PACK)
        ]
        m0 = [sbuf("m0_%d" % b, U, F32) for b in range(2)]
        m1 = [sbuf("m1_%d" % b, U, F32) for b in range(2)]

        for tile in (wb_s, wo_s):
            nc.vector.memset(tile[:].bitcast(I32), 0)
        for tile in m0:
            nc.gpsimd.memset(tile[:], 0.0)
        for tile in page[-1:] + m1:
            nc.vector.memset(tile[:], 0.0)

        l2 = load_list("l2", offs2)
        load_scale_window(wts_win, wt_scales)
        load_bytes(wt_win, wt_words[0])
        l1 = load_list("l1", offs)
        load_scale_window(xts_win, xt_scales)
        load_bytes(xt_win, xt_words[0])
        l3 = load_list("l3", offs3)
        nc.sync.dma_start(sa_t[:], sa.rearrange("(p t) o -> p (t o)", t=PACK))
        l5 = load_list("l5", offs5)
        nc.sync.dma_start(sb_t[:], sb.rearrange("(p t) o -> p (t o)", t=PACK))
        l4 = load_list("l4", offs4)
        load_bytes(wb_w, wb_words[0].rearrange("p n t -> p (n t)"))
        load_scale_rows(wb_s, wb_scales)
        l6 = load_list("l6", offs6)
        load_bytes(wo_w, wo_words[0])
        load_scale_rows(wo_s, wo_scales)
        l7 = load_list("l7", offs7)

        wt_g = sbuf("wt_g", R, U16)
        wts_g = sbuf("wts_g", R, U8)
        xt_g = sbuf("xt_g", J, U16)
        xts_g = sbuf("xts_g", J, U8)
        nc.vector.tensor_copy(wts_g[:], wts_win[:].indirect(l2[:]))
        nc.vector.tensor_copy(wt_g[:], wt_win[:].indirect(l2[:]))
        nc.vector.tensor_copy(xts_g[:], xts_win[:].indirect(l1[:]))

        def deal(t):
            if t == 0:
                words = sbuf("wt_d0", 2 * P, U8)
                scales = sbuf("wts_d0", P, U8)
            else:
                scales = reuse.tile([P, P], U8, name="wts_d%d" % t, align_bytes=64, offset=2 * PAGE_BYTES + (t + 1) * P)
                words = reuse.tile([P, 2 * P], U8, name="wt_d%d" % t, align_bytes=64, offset=max(PAGE_BYTES - 2 * P, (t - 1) * PAGE_BYTES))
            nc.vector.tensor_copy(words[:].bitcast(U16), wt_g[:].rearrange("p (m t) -> p m t", t=PACK)[:, :, t])
            nc.vector.tensor_copy(scales[:], wts_g[:].rearrange("p (m t) -> p m t", t=PACK)[:, :, t])
            return words, scales

        def first_product(acc, lhs, cols):
            nc.tensor.matmul_mx(
                out=acc, lhsT=lhs[0][:].bitcast(FP4X4), lhsT_scale=lhs[1][:],
                rhs=xt_g[:, cols].bitcast(FP4X4), rhs_scale=xts_g[:, cols], start=True, stop=True,
            )

        a = [sbuf("a%d" % t, J, F32) for t in range(PACK)]
        lhs0 = deal(0)
        for s in range(2):
            cols = slice(s * JH, (s + 1) * JH)
            nc.vector.tensor_copy(xt_g[:, cols], xt_win[:].indirect(l1[:, s * JH // 16 : (s + 1) * JH // 16]))
            acc = psum.tile([P, JH], F32, name="acc0_%d" % s)
            first_product(acc[:], lhs0, cols)
            nc.scalar.copy(a[0][:, cols], acc[:])

        hid = [sbuf("hid%d" % s, PACK * HALF, BF16, tag="diff" if s == 0 else "") for s in range(2)]
        codes = sbuf("codes", C, U32)
        planes = sbuf("planes", C, U8)

        def second_fetch(dst, t, s):
            nc.scalar.activation(
                out=dst, in_=a[t][:].indirect(l5[:, s * HALF // 16 : (s + 1) * HALF // 16]), func=COPY,
                scale=sb_t[:, t : t + 1],
            )

        for t in range(1, PACK):
            lhs = deal(t)
            acc = psum.tile([P, J], F32, name="acc%d" % t)
            first_product(acc[:], lhs, slice(0, J))
            nc.vector.tensor_copy(a[t][:], acc[:])
            nc.vector.memset(page[t - 1][:], 0.0)

        def first_fetch(t):
            h1 = sbuf("h1_%d" % t, O, F32, tag="late" if t == PACK - 1 else "")
            nc.scalar.activation(out=h1[:], in_=a[t][:].indirect(l3[:]), func=COPY, scale=sa_t[:, t : t + 1])
            return h1

        ahead = first_fetch(0)
        for t in range(PACK):
            h1 = ahead
            g = sbuf("gA%d" % t, HALF, F32)
            second_fetch(g[:], t, 0)
            if t + 1 < PACK:
                ahead = first_fetch(t + 1)
            nc.scalar.activation(out=page[t][:].indirect(l4[:]), in_=h1[:], func=COPY)
            d = sbuf("dA%d" % t, HALF, F32)
            nc.vector.tensor_tensor(d[:], page[t][:, 0:HALF], g[:], ALU.subtract)
            nc.vector.scalar_tensor_tensor(
                out=hid[0][:].rearrange("p (c t) -> p c t", t=PACK)[:, :, t], in0=d[:], scalar=-1.0, in1=d[:],
                op0=ALU.mult, op1=ALU.max,
            )

        gB = sbuf("gB", PACK * HALF, F32, tag="late")
        for t in range(PACK):
            second_fetch(gB[:, t * HALF : (t + 1) * HALF], t, 1)

        first = (wb_w, wb_s, FP8X4, m0, l6)
        second = (wo_w, wo_s, FP4X4, m1, l7)

        def quantise(s):
            cols = slice(s * HALF, (s + 1) * HALF)
            nc.vector.quantize_mx(out=codes[:, cols].bitcast(FP8X4), scales=planes[:, cols], in_=hid[s][:])

        def product(outcome, b, cols, acc):
            words, scales, fmt = outcome[:3]
            rows = slice(b * P, (b + 1) * P)
            nc.tensor.matmul_mx(
                out=acc, lhsT=words[:, rows].bitcast(fmt), lhsT_scale=scales[:, rows],
                rhs=codes[:, cols].bitcast(FP8X4), rhs_scale=planes[:, cols], start=True, stop=True,
            )

        def put(outcome, b, cols, res):
            window, lst = outcome[3][b], outcome[4]
            nc.scalar.activation(
                out=window[:].indirect(lst[:, cols.start // 16 : cols.stop // 16]), in_=res, func=COPY
            )

        def bucket_tops(outcome, b, name):
            top = sbuf(name, E, F32)
            nc.vector.tensor_reduce(
                out=top[:], in_=outcome[3][b][:].rearrange("p (e u) -> p e u", u=U // E),
                axis=mybir.AxisListType.X, op=ALU.max,
            )
            return top

        left, right, whole = slice(0, HALF), slice(HALF, C), slice(0, C)
        early = [(first, 0), (second, 0), (first, 1)]
        quantise(0)
        accs = [psum.tile([P, HALF], F32, name="early%d" % i) for i in range(len(early))]
        for acc, (o, b) in zip(accs, early):
            product(o, b, left, acc[:])
        lead = sbuf("lead", HALF, F32)
        nc.scalar.copy(lead[:], accs[0][:])
        put(first, 0, left, lead[:])

        dB = sbuf("dB", PACK * HALF, F32, tag="diff")
        for t in range(PACK):
            cols = slice(t * HALF, (t + 1) * HALF)
            nc.vector.tensor_tensor(dB[:, cols], page[t][:, right], gB[:, cols], ALU.subtract)
        dB_ct = dB[:].rearrange("p (t c) -> p c t", t=PACK)
        nc.vector.scalar_tensor_tensor(
            out=hid[1][:].rearrange("p (c t) -> p c t", t=PACK), in0=dB_ct, scalar=-1.0, in1=dB_ct,
            op0=ALU.mult, op1=ALU.max,
        )
        resA = sbuf("resA", 2 * HALF, F32, tag="late")
        nc.vector.tensor_copy(resA[:, left], accs[1][:])
        put(second, 0, left, resA[:, left])
        quantise(1)
        nc.vector.tensor_copy(resA[:, right], accs[2][:])
        put(first, 1, left, resA[:, right])

        accB = psum.tile([P, len(early) * HALF], F32, name="accB", tag="acc1")
        for i, (o, b) in enumerate(early):
            product(o, b, right, accB[:, i * HALF : (i + 1) * HALF])
        resB = sbuf("resB", len(early) * HALF, F32)
        nc.vector.tensor_copy(resB[:], accB[:])
        accW = psum.tile([P, C], F32, name="accW", tag="acc2")
        product(second, 1, whole, accW[:])
        resW = sbuf("resW", C, F32)
        nc.vector.tensor_copy(resW[:], accW[:])

        late = [(o, b, right, resB[:, i * HALF : (i + 1) * HALF]) for i, (o, b) in enumerate(early)]
        tops = []
        for i, (o, b, cols, res) in enumerate(late + [(second, 1, whole, resW[:])]):
            put(o, b, cols, res)
            tops.append(bucket_tops(o, b, "top%d" % i))
            if o is second:
                y = sbuf("y%d" % b, E, F32)
                nc.vector.tensor_tensor(y[:], tops[-2][:], tops[-1][:], ALU.subtract)
                nc.sync.dma_start(out[b * P : (b + 1) * P, :], y[:])
